import numpy as np
import ml_dtypes


def mxq(x, axis, fmt="e4m3"):
    dtype, down = {"e4m3": (ml_dtypes.float8_e4m3fn, 7), "e5m2": (ml_dtypes.float8_e5m2, 14)}[fmt]
    v = np.moveaxis(np.asarray(x, np.float32).astype(ml_dtypes.bfloat16).astype(np.float64), axis, -1)
    blocks = v.reshape(v.shape[:-1] + (-1, 32))
    amax = np.abs(blocks).max(-1, keepdims=True)
    byte = np.maximum(np.where(amax > 0, np.frexp(amax)[1] - 1 + 127, 0) - down, 1)
    scale = np.exp2(byte - 127.0)
    codes = (blocks / scale).astype(np.float32).astype(dtype).astype(np.float64)
    return np.moveaxis((codes * scale).reshape(v.shape), -1, axis)


WIDE = False


def mx_kscale(k, group=512):
    if not WIDE:
        return np.ones(k)
    levels = np.array([10, -10, 5, -5, 0])
    if group != 512:
        return np.exp2(np.random.permutation(np.resize(levels, k // group))).repeat(group)
    if k % 512:
        return np.exp2(np.random.permutation(np.resize(levels, k // 32))).repeat(32)
    a = np.empty((k // 512, 16))
    for p in range(k // 512):
        a[p, :8] = np.random.permutation(np.resize(levels, 8))
        for g in range(8):
            far = levels[np.abs(levels - a[p, g]) >= 10]
            a[p, g + 8] = far[np.random.randint(len(far))]
    return np.exp2(a.ravel()).repeat(32)


def f64(x):
    return np.asarray(x).astype(np.float64)


def sigmoid(v):
    return 1.0 / (1.0 + np.exp(-v))


G, D, M, O, N = 2, 256, 128, 256, 512


def setup_inputs():
    n = np.random.standard_normal
    s_d = mx_kscale(D, 0)
    s_o = mx_kscale(O, 0)
    return {
        "x": (n((G, D, N)) * s_d[:, None]).astype(np.float32),
        "w1": (n((G, D, M)) / np.sqrt(D) / s_d[:, None]).astype(np.float32),
        "w2": (n((G, D, M)) / np.sqrt(D) / s_d[:, None]).astype(np.float32),
        "w3": (n((G, D, M)) / np.sqrt(D) / s_d[:, None]).astype(np.float32),
        "th": (0.5 * n((G, M, 1))).astype(np.float32),
        "wo": (n((G, O, M)) / np.sqrt(O) / s_o[:, None]).astype(np.float32),
        "dy": (n((G, O, N)) * s_o[:, None]).astype(np.float32),
        "dx": (n((G, D, N)) * s_d[:, None]).astype(np.float32),
        "og": (np.random.uniform(0.5, 2.0, (G, M, 1))).astype(np.float32),
        "base": (0.3 * n((G, M, N))).astype(np.float32),
    }


def reference(x, w1, w2, w3, th, wo, dy, dx, og, base):
    w1q = mxq(f64(w1), 1, "e4m3")
    xq = mxq(f64(x), 1, "e4m3")
    z1 = w1q.transpose(0, 2, 1) @ xq
    dxq = mxq(f64(dx), 1, "e4m3")
    tz1 = w1q.transpose(0, 2, 1) @ dxq
    w2q = mxq(f64(w2), 1, "e4m3")
    z2 = w2q.transpose(0, 2, 1) @ xq
    tz2 = w2q.transpose(0, 2, 1) @ dxq
    w3q = mxq(f64(w3), 1, "e4m3")
    z3 = w3q.transpose(0, 2, 1) @ xq
    tz3 = w3q.transpose(0, 2, 1) @ dxq
    g2 = sigmoid(z2)
    g3 = sigmoid(z3 - f64(th))
    woq = mxq(f64(wo), 1, "e4m3")
    dyq = mxq(f64(dy), 1, "e4m3")
    c0 = woq.transpose(0, 2, 1) @ dyq
    dg2 = c0 * g3 * z1
    xg2 = tz2 * g2 * (1.0 - g2)
    xg3 = tz3 * g3 * (1.0 - g3)
    xdg2 = xg3 * c0 * z1 + tz1 * c0 * g3
    xdz2 = (xdg2 * g2 + xg2 * dg2) * (1.0 - g2) + xg2 * (-1.0) * dg2 * g2
    y = xdz2 * f64(og) + f64(base)
    return y

@@ -1,0 +1,189 @@
+from contextlib import ExitStack
+
+import concourse.mybir as mybir
+
+G, D, M, N = 2, 256, 128, 512
+FLOPS = 7 * 2 * G * D * M * N
+
+F32 = mybir.dt.float32
+BF16 = mybir.dt.bfloat16
+U32 = mybir.dt.uint32
+U8 = mybir.dt.uint8
+FP8X4 = mybir.dt.float8_e4m3fn_x4
+ALU = mybir.AluOpType
+ACT = mybir.ActivationFunctionType
+
+P = 128
+PACK = 4
+ROWS = D // PACK
+HALF = N // 2
+RUN = 4
+
+
+def tile_rows_hvtwogates_kernel(tc, x, w1, w2, w3, th, wo, dy, dx, og, base, out):
+    nc = tc.nc
+
+    with ExitStack() as ctx:
+        sb = ctx.enter_context(tc.tile_pool(name="sb", bufs=1))
+        ps = ctx.enter_context(tc.psum_pool(name="ps", bufs=1))
+        ctx.enter_context(tc.manual_schedule())
+
+        def load(name, src, c0, c1):
+            raw = sb.tile([P, PACK, c1 - c0], F32, name=name)
+            nc.sync.dma_start(out=raw[:], in_=src.rearrange("g (p j) n -> (g p) j n", j=PACK)[:, :, c0:c1])
+            return raw
+
+        def operand(name, width):
+            rounded = sb.tile([P, width, PACK], BF16, name=name + "_bf", align_bytes=64)
+            codes = sb.tile([P, width], U32, name=name + "_codes", align_bytes=64)
+            scales = sb.tile([P, width], U8, name=name + "_scales", align_bytes=64)
+            return rounded, codes, scales
+
+        def views(op, at, raw, c0, c1):
+            dst = op[0][:, at + c0 : at + c1, :].rearrange("p (c i) j -> p c j i", i=RUN)
+            src = raw[:, :, c0:c1].rearrange("p j (c i) -> p c j i", i=RUN)
+            return dst, src
+
+        def round_v(op, at, raw, c0, c1):
+            dst, src = views(op, at, raw, c0, c1)
+            nc.vector.tensor_copy(out=dst, in_=src)
+
+        def round_s(op, at, raw, c0, c1):
+            dst, src = views(op, at, raw, c0, c1)
+            nc.scalar.activation(out=dst, in_=src, func=ACT.Copy)
+
+        def quantise(op, c0, c1):
+            nc.vector.quantize_mx(
+                out=op[1][:, c0:c1].bitcast(FP8X4),
+                scales=op[2][:, c0:c1],
+                in_=op[0][:, c0:c1, :].rearrange("p c j -> p (c j)"),
+            )
+
+        def product(bank, g, w, a):
+            rows = slice(g * ROWS, (g + 1) * ROWS)
+            nc.tensor.matmul_mx(
+                out=bank[:],
+                lhsT=w[1][rows, :].bitcast(FP8X4),
+                lhsT_scale=w[2][rows, :],
+                rhs=a[1][rows, :].bitcast(FP8X4),
+                rhs_scale=a[2][rows, :],
+                start=True,
+                stop=True,
+            )
+
+        th_sb = sb.tile([P, G], F32, name="th_sb")
+        og_sb = sb.tile([P, G], F32, name="og_sb")
+        with nc.allow_non_contiguous_dma(reason="one value a partition and group"):
+            nc.scalar.dma_start(out=th_sb[:], in_=th.rearrange("g m o -> m (g o)"))
+            nc.scalar.dma_start(out=og_sb[:], in_=og.rearrange("g m o -> m (g o)"))
+        x0 = load("x0", x, 0, HALF)
+        dx0 = load("dx0", dx, 0, HALF)
+        w3r = load("w3r", w3, 0, M)
+        w2r = load("w2r", w2, 0, M)
+        w1r = load("w1r", w1, 0, M)
+        x1 = load("x1", x, HALF, N)
+        dx1 = load("dx1", dx, HALF, N)
+        wor = load("wor", wo, 0, M)
+        dyr = load("dyr", dy, 0, N)
+        base_sb = sb.tile([P, G, N], F32, name="base_sb")
+        nc.sync.dma_start(out=base_sb[:], in_=base.rearrange("g m n -> m g n"))
+
+        bias3 = sb.tile([P, G], F32, name="bias3")
+        nc.gpsimd.tensor_scalar(out=bias3[:], in0=th_sb[:], scalar1=-0.5, scalar2=0.0, op0=ALU.mult, op1=ALU.add)
+
+        pair = [operand("pair%d" % h, N) for h in range(2)]
+        w1q, w2q, w3q, woq = [operand(n, M) for n in ("w1", "w2", "w3", "wo")]
+        dyq = operand("dy", N)
+
+        bank1 = [ps.tile([P, N], F32, name="bank1_%d" % g) for g in range(G)]
+        bank2 = [ps.tile([P, N], F32, name="bank2_%d" % g) for g in range(G)]
+        bank3 = [ps.tile([P, N], F32, name="bank3_%d" % g) for g in range(G)]
+        bankc = [ps.tile([P, N], F32, name="bankc_%d" % g) for g in range(G)]
+
+        def work(name):
+            return [[sb.tile([P, HALF], F32, name="%s_%d_%d" % (name, h, g)) for g in range(G)] for h in range(2)]
+
+        t2, t3, sq, va, vb, vc, vd, ve, vf = [work(n) for n in ("t2", "t3", "sq", "va", "vb", "vc", "vd", "ve", "vf")]
+        res = [sb.tile([P, N], F32, name="res%d" % g) for g in range(G)]
+        fin = [sb.tile([P, N], F32, name="fin%d" % g) for g in range(G)]
+        outs = [sb.tile([P, N], F32, name="outs%d" % g) for g in range(G)]
+        lo = slice(0, HALF)
+        hi = slice(HALF, N)
+
+        def stt(o, a, s, b, op0, op1):
+            nc.vector.scalar_tensor_tensor(out=o, in0=a, scalar=s, in1=b, op0=op0, op1=op1)
+
+        def gates(h):
+            for g in range(G):
+                nc.scalar.activation(out=t3[h][g][:], in_=bank3[g][:, lo], func=ACT.Tanh, scale=0.5, bias=bias3[:, g : g + 1])
+            for g in range(G):
+                nc.scalar.activation(out=t2[h][g][:], in_=bank2[g][:, lo], func=ACT.Tanh, scale=0.5)
+
+        def squares(h):
+            for g in range(G):
+                nc.scalar.activation(out=sq[h][g][:], in_=t2[h][g][:], func=ACT.Square)
+
+        def bracket(h):
+            for g in range(G):
+                stt(va[h][g][:], t3[h][g][:], 1.0, bank3[g][:, hi], ALU.subtract, ALU.mult)
+            for g in range(G):
+                stt(vb[h][g][:], t2[h][g][:], 2.0, bank2[g][:, hi], ALU.mult, ALU.mult)
+            for g in range(G):
+                nc.vector.tensor_tensor(out=vc[h][g][:], in0=va[h][g][:], in1=vb[h][g][:], op=ALU.add)
+            for g in range(G):
+                stt(vd[h][g][:], vc[h][g][:], 0.5, bank1[g][:, lo], ALU.mult, ALU.mult)
+            for g in range(G):
+                nc.vector.tensor_tensor(out=ve[h][g][:], in0=vd[h][g][:], in1=bank1[g][:, hi], op=ALU.subtract)
+
+        def times_g3(h):
+            for g in range(G):
+                stt(vf[h][g][:], t3[h][g][:], 1.0, ve[h][g][:], ALU.add, ALU.mult)
+
+        def times_slope(h):
+            for g in range(G):
+                stt(res[g][:, h * HALF : (h + 1) * HALF], sq[h][g][:], 1.0, vf[h][g][:], ALU.subtract, ALU.mult)
+
+        gain = sb.tile([P, G], F32, name="gain")
+        nc.gpsimd.tensor_scalar(out=gain[:], in0=og_sb[:], scalar1=0.125, scalar2=0.0, op0=ALU.mult, op1=ALU.add)
+
+        SPLIT = 160
+        round_v(pair[0], 0, x0, 0, SPLIT)
+        round_s(pair[0], 0, x0, SPLIT, HALF)
+        quantise(pair[0], 0, HALF)
+        round_v(pair[0], HALF, dx0, 0, SPLIT)
+        round_s(pair[0], HALF, dx0, SPLIT, HALF)
+        quantise(pair[0], HALF, N)
+        for wq, wr, bank in ((w3q, w3r, bank3), (w2q, w2r, bank2), (w1q, w1r, bank1)):
+            round_v(wq, 0, wr, 0, M)
+            quantise(wq, 0, M)
+            for g in range(G):
+                product(bank[g], g, wq, pair[0])
+        gates(0)
+        bracket(0)
+        round_s(pair[1], 0, x1, 0, HALF)
+        squares(0)
+        round_v(pair[1], HALF, dx1, 0, 128)
+        round_s(pair[1], HALF, dx1, 128, HALF)
+        quantise(pair[1], 0, HALF)
+        quantise(pair[1], HALF, N)
+        for wq, bank in ((w3q, bank3), (w2q, bank2), (w1q, bank1)):
+            for g in range(G):
+                product(bank[g], g, wq, pair[1])
+        round_s(woq, 0, wor, 0, M)
+        times_g3(0)
+        times_slope(0)
+        quantise(woq, 0, M)
+        gates(1)
+        bracket(1)
+        round_s(dyq, 0, dyr, 0, N)
+        squares(1)
+        quantise(dyq, 0, N)
+        for g in range(G):
+            product(bankc[g], g, woq, dyq)
+        times_g3(1)
+        times_slope(1)
+        for g in range(G):
+            stt(fin[g][:], bankc[g][:], gain[:, g : g + 1], res[g][:], ALU.mult, ALU.mult)
+        for g in range(G):
+            nc.vector.tensor_tensor(out=outs[g][:], in0=fin[g][:], in1=base_sb[:, g, :], op=ALU.add)
+            nc.sync.dma_start(out=out[g], in_=outs[g][:])

@@ -17,7 +17,9 @@ P = 128
 PACK = 4
 ROWS = D // PACK
 HALF = N // 2
-RUN = 4
+RUN = 2
+QUAD = 32
+NT = 128
 
 
 def tile_rows_hvtwogates_kernel(tc, x, w1, w2, w3, th, wo, dy, dx, og, base, out):
@@ -59,27 +61,30 @@ def tile_rows_hvtwogates_kernel(tc, x, w1, w2, w3, th, wo, dy, dx, og, base, out
                 in_=op[0][:, c0:c1, :].rearrange("p c j -> p (c j)"),
             )
 
-        def product(bank, g, w, a):
+        def product(bank, at, g, w, a):
             rows = slice(g * ROWS, (g + 1) * ROWS)
-            nc.tensor.matmul_mx(
-                out=bank[:],
-                lhsT=w[1][rows, :].bitcast(FP8X4),
-                lhsT_scale=w[2][rows, :],
-                rhs=a[1][rows, :].bitcast(FP8X4),
-                rhs_scale=a[2][rows, :],
-                start=True,
-                stop=True,
-            )
+            for n0 in range(0, a[1].shape[1], NT):
+                nc.tensor.matmul_mx(
+                    out=bank[g][:, at + n0 : at + n0 + NT],
+                    lhsT=w[1][rows, :].bitcast(FP8X4),
+                    lhsT_scale=w[2][rows, :],
+                    rhs=a[1][rows, n0 : n0 + NT].bitcast(FP8X4),
+                    rhs_scale=a[2][rows, n0 : n0 + NT],
+                    start=True,
+                    stop=True,
+                )
 
-        th_sb = sb.tile([P, G], F32, name="th_sb")
-        og_sb = sb.tile([P, G], F32, name="og_sb")
-        with nc.allow_non_contiguous_dma(reason="one value a partition and group"):
-            nc.scalar.dma_start(out=th_sb[:], in_=th.rearrange("g m o -> m (g o)"))
-            nc.scalar.dma_start(out=og_sb[:], in_=og.rearrange("g m o -> m (g o)"))
+        rows_in = sb.tile([P, 2 * G, QUAD], F32, name="rows_in", align_bytes=64)
+        cols = sb.tile([P, 2 * G, QUAD], F32, name="cols", align_bytes=64)
+        nc.gpsimd.memset(rows_in[:], 0.0)
+        for r, vec in enumerate((th, og)):
+            nc.scalar.dma_start(
+                out=rows_in[0:P:QUAD, r * G : (r + 1) * G, :], in_=vec.rearrange("g (q i) o -> q g (i o)", i=QUAD)
+            )
         x0 = load("x0", x, 0, HALF)
+        w2r = load("w2r", w2, 0, M)
         dx0 = load("dx0", dx, 0, HALF)
         w3r = load("w3r", w3, 0, M)
-        w2r = load("w2r", w2, 0, M)
         w1r = load("w1r", w1, 0, M)
         x1 = load("x1", x, HALF, N)
         dx1 = load("dx1", dx, HALF, N)
@@ -89,101 +94,141 @@ def tile_rows_hvtwogates_kernel(tc, x, w1, w2, w3, th, wo, dy, dx, og, base, out
         nc.sync.dma_start(out=base_sb[:], in_=base.rearrange("g m n -> m g n"))
 
         bias3 = sb.tile([P, G], F32, name="bias3")
-        nc.gpsimd.tensor_scalar(out=bias3[:], in0=th_sb[:], scalar1=-0.5, scalar2=0.0, op0=ALU.mult, op1=ALU.add)
-
-        pair = [operand("pair%d" % h, N) for h in range(2)]
+        xq = [operand("x%d" % h, HALF) for h in range(2)]
+        dxq = [operand("dx%d" % h, HALF) for h in range(2)]
         w1q, w2q, w3q, woq = [operand(n, M) for n in ("w1", "w2", "w3", "wo")]
-        dyq = operand("dy", N)
+        dyq = [operand("dy%d" % h, HALF) for h in range(2)]
 
-        bank1 = [ps.tile([P, N], F32, name="bank1_%d" % g) for g in range(G)]
-        bank2 = [ps.tile([P, N], F32, name="bank2_%d" % g) for g in range(G)]
-        bank3 = [ps.tile([P, N], F32, name="bank3_%d" % g) for g in range(G)]
-        bankc = [ps.tile([P, N], F32, name="bankc_%d" % g) for g in range(G)]
+        gate_sums, tan3, tan2, values = [
+            [ps.tile([P, N], F32, name="%s_%d" % (n, g)) for g in range(G)] for n in ("gate_sums", "tan3", "tan2", "values")
+        ]
+        bankc = tan3
 
         def work(name):
-            return [[sb.tile([P, HALF], F32, name="%s_%d_%d" % (name, h, g)) for g in range(G)] for h in range(2)]
+            return [sb.tile([P, G, HALF], F32, name="%s_%d" % (name, h)) for h in range(2)]
 
         t2, t3, sq, va, vb, vc, vd, ve, vf = [work(n) for n in ("t2", "t3", "sq", "va", "vb", "vc", "vd", "ve", "vf")]
-        res = [sb.tile([P, N], F32, name="res%d" % g) for g in range(G)]
-        fin = [sb.tile([P, N], F32, name="fin%d" % g) for g in range(G)]
-        outs = [sb.tile([P, N], F32, name="outs%d" % g) for g in range(G)]
+        res = sb.tile([P, G, N], F32, name="res")
+        fin = sb.tile([P, G, N], F32, name="fin")
+        outs = sb.tile([P, G, N], F32, name="outs")
         lo = slice(0, HALF)
         hi = slice(HALF, N)
 
         def stt(o, a, s, b, op0, op1):
             nc.vector.scalar_tensor_tensor(out=o, in0=a, scalar=s, in1=b, op0=op0, op1=op1)
 
-        def gates(h):
-            for g in range(G):
-                nc.scalar.activation(out=t3[h][g][:], in_=bank3[g][:, lo], func=ACT.Tanh, scale=0.5, bias=bias3[:, g : g + 1])
-            for g in range(G):
-                nc.scalar.activation(out=t2[h][g][:], in_=bank2[g][:, lo], func=ACT.Tanh, scale=0.5)
+        def tanh3(h, g):
+            nc.scalar.activation(out=t3[h][:, g, :], in_=gate_sums[g][:, lo], func=ACT.Tanh, scale=0.5, bias=bias3[:, g : g + 1])
+
+        def tanh2(h, g):
+            nc.scalar.activation(out=t2[h][:, g, :], in_=gate_sums[g][:, hi], func=ACT.Tanh, scale=0.5)
 
         def squares(h):
-            for g in range(G):
-                nc.scalar.activation(out=sq[h][g][:], in_=t2[h][g][:], func=ACT.Square)
+            nc.scalar.activation(out=sq[h][:], in_=t2[h][:], func=ACT.Square, scale=0.5)
+
+        def term3(h, gs):
+            for g in gs:
+                stt(va[h][:, g, :], t3[h][:, g, :], 1.0, tan3[g][:, lo], ALU.subtract, ALU.mult)
+
+        def term2(h, gs):
+            for g in gs:
+                stt(vb[h][:, g, :], t2[h][:, g, :], 2.0, tan2[g][:, lo], ALU.mult, ALU.mult)
+
+        def term_sum(h):
+            nc.vector.tensor_tensor(out=vc[h][:], in0=va[h][:], in1=vb[h][:], op=ALU.add)
 
         def bracket(h):
             for g in range(G):
-                stt(va[h][g][:], t3[h][g][:], 1.0, bank3[g][:, hi], ALU.subtract, ALU.mult)
+                stt(vd[h][:, g, :], vc[h][:, g, :], 0.25, values[g][:, lo], ALU.mult, ALU.mult)
             for g in range(G):
-                stt(vb[h][g][:], t2[h][g][:], 2.0, bank2[g][:, hi], ALU.mult, ALU.mult)
-            for g in range(G):
-                nc.vector.tensor_tensor(out=vc[h][g][:], in0=va[h][g][:], in1=vb[h][g][:], op=ALU.add)
-            for g in range(G):
-                stt(vd[h][g][:], vc[h][g][:], 0.5, bank1[g][:, lo], ALU.mult, ALU.mult)
-            for g in range(G):
-                nc.vector.tensor_tensor(out=ve[h][g][:], in0=vd[h][g][:], in1=bank1[g][:, hi], op=ALU.subtract)
+                stt(ve[h][:, g, :], values[g][:, hi], 0.5, vd[h][:, g, :], ALU.mult, ALU.subtract)
 
-        def times_g3(h):
-            for g in range(G):
-                stt(vf[h][g][:], t3[h][g][:], 1.0, ve[h][g][:], ALU.add, ALU.mult)
+        def times_g3(h, gs):
+            stt(vf[h][:, gs, :], t3[h][:, gs, :], 1.0, ve[h][:, gs, :], ALU.add, ALU.mult)
 
-        def times_slope(h):
-            for g in range(G):
-                stt(res[g][:, h * HALF : (h + 1) * HALF], sq[h][g][:], 1.0, vf[h][g][:], ALU.subtract, ALU.mult)
-
-        gain = sb.tile([P, G], F32, name="gain")
-        nc.gpsimd.tensor_scalar(out=gain[:], in0=og_sb[:], scalar1=0.125, scalar2=0.0, op0=ALU.mult, op1=ALU.add)
+        def times_slope(h, gs):
+            stt(res[:, gs, h * HALF : (h + 1) * HALF], sq[h][:, gs, :], 0.25, vf[h][:, gs, :], ALU.subtract, ALU.mult)
 
         SPLIT = 160
-        round_v(pair[0], 0, x0, 0, SPLIT)
-        round_s(pair[0], 0, x0, SPLIT, HALF)
-        quantise(pair[0], 0, HALF)
-        round_v(pair[0], HALF, dx0, 0, SPLIT)
-        round_s(pair[0], HALF, dx0, SPLIT, HALF)
-        quantise(pair[0], HALF, N)
-        for wq, wr, bank in ((w3q, w3r, bank3), (w2q, w2r, bank2), (w1q, w1r, bank1)):
-            round_v(wq, 0, wr, 0, M)
-            quantise(wq, 0, M)
-            for g in range(G):
-                product(bank[g], g, wq, pair[0])
-        gates(0)
-        bracket(0)
-        round_s(pair[1], 0, x1, 0, HALF)
+        both = slice(0, G)
+        round_v(xq[0], 0, x0, 0, SPLIT)
+        round_s(xq[0], 0, x0, SPLIT, HALF)
+        round_s(w2q, 0, w2r, 0, M)
+        quantise(xq[0], 0, HALF)
+        quantise(w2q, 0, M)
+        for g in range(G):
+            product(gate_sums, HALF, g, w2q, xq[0])
+        round_v(dxq[0], 0, dx0, 0, SPLIT)
+        round_s(dxq[0], 0, dx0, SPLIT, HALF)
+        for g in range(G):
+            tanh2(0, g)
         squares(0)
-        round_v(pair[1], HALF, dx1, 0, 128)
-        round_s(pair[1], HALF, dx1, 128, HALF)
-        quantise(pair[1], 0, HALF)
-        quantise(pair[1], HALF, N)
-        for wq, bank in ((w3q, bank3), (w2q, bank2), (w1q, bank1)):
-            for g in range(G):
-                product(bank[g], g, wq, pair[1])
+        quantise(dxq[0], 0, HALF)
+        for g in range(G):
+            product(tan2, 0, g, w2q, dxq[0])
+        round_v(w3q, 0, w3r, 0, M)
+        nc.vector.transpose(out=cols[:].rearrange("p b i -> p (b i)"), in_=rows_in[:].rearrange("p b i -> p (b i)"))
+        quantise(w3q, 0, M)
+        round_s(w1q, 0, w1r, 0, M)
+        nc.scalar.activation(out=bias3[:], in_=cols[:, 0:G, 0], func=ACT.Copy, scale=-0.5)
+        for g in range(G):
+            product(gate_sums, 0, g, w3q, xq[0])
+            product(tan3, 0, g, w3q, dxq[0])
+        term2(0, range(G))
+        quantise(w1q, 0, M)
+        for g in range(G):
+            tanh3(0, g)
+        for g in range(G):
+            product(values, 0, g, w1q, xq[0])
+            product(values, HALF, g, w1q, dxq[0])
+        term3(0, range(G))
+        round_s(xq[1], 0, x1, 0, HALF)
+        round_s(dxq[1], 0, dx1, 0, HALF)
+        for g in range(G):
+            nc.vector.tensor_tensor(out=vc[0][:, g, :], in0=va[0][:, g, :], in1=vb[0][:, g, :], op=ALU.add)
+        quantise(xq[1], 0, HALF)
+        for g in range(G):
+            product(gate_sums, 0, g, w3q, xq[1])
+            product(gate_sums, HALF, g, w2q, xq[1])
+        bracket(0)
+        quantise(dxq[1], 0, HALF)
+        for g in range(G):
+            product(tan3, 0, g, w3q, dxq[1])
+            product(tan2, 0, g, w2q, dxq[1])
+        for g in range(G):
+            product(values, 0, g, w1q, xq[1])
+            product(values, HALF, g, w1q, dxq[1])
+        for g in range(G):
+            tanh3(1, g)
+            tanh2(1, g)
         round_s(woq, 0, wor, 0, M)
-        times_g3(0)
-        times_slope(0)
+        times_g3(0, both)
+        for g in range(G):
+            term3(1, [g])
+            term2(1, [g])
+        times_slope(0, both)
         quantise(woq, 0, M)
-        gates(1)
-        bracket(1)
-        round_s(dyq, 0, dyr, 0, N)
+        for h in range(2):
+            round_s(dyq[h], -h * HALF, dyr, h * HALF, (h + 1) * HALF)
         squares(1)
-        quantise(dyq, 0, N)
+        quantise(dyq[0], 0, HALF)
         for g in range(G):
-            product(bankc[g], g, woq, dyq)
-        times_g3(1)
-        times_slope(1)
+            product(bankc, 0, g, woq, dyq[0])
+        term_sum(1)
         for g in range(G):
-            stt(fin[g][:], bankc[g][:], gain[:, g : g + 1], res[g][:], ALU.mult, ALU.mult)
+            stt(fin[:, g, lo], bankc[g][:, lo], cols[:, G + g, 0:1], res[:, g, lo], ALU.mult, ALU.mult)
+            nc.gpsimd.tensor_tensor(out=outs[:, g, lo], in0=base_sb[:, g, lo], in1=fin[:, g, lo], op=ALU.subtract)
+        nc.sync.dma_start(out=out.rearrange("g m n -> m g n")[:, :, lo], in_=outs[:, :, lo])
+        bracket(1)
+        quantise(dyq[1], 0, HALF)
         for g in range(G):
-            nc.vector.tensor_tensor(out=outs[g][:], in0=fin[g][:], in1=base_sb[:, g, :], op=ALU.add)
-            nc.sync.dma_start(out=out[g], in_=outs[g][:])
+            product(bankc, HALF, g, woq, dyq[1])
+        for g in range(G):
+            times_g3(1, slice(g, g + 1))
+        for g in range(G):
+            times_slope(1, slice(g, g + 1))
+        for g in range(G):
+            stt(fin[:, g, hi], bankc[g][:, hi], cols[:, G + g, 0:1], res[:, g, hi], ALU.mult, ALU.mult)
+        for g, queue in ((0, nc.scalar), (1, nc.sync)):
+            nc.vector.tensor_tensor(out=outs[:, g, hi], in0=base_sb[:, g, hi], in1=fin[:, g, hi], op=ALU.subtract)
+            queue.dma_start(out=out[g, :, hi], in_=outs[:, g, hi])

from contextlib import ExitStack

import concourse.mybir as mybir

G, D, M, N = 2, 256, 128, 512
FLOPS = 7 * 2 * G * D * M * N

F32 = mybir.dt.float32
BF16 = mybir.dt.bfloat16
U32 = mybir.dt.uint32
U8 = mybir.dt.uint8
FP8X4 = mybir.dt.float8_e4m3fn_x4
ALU = mybir.AluOpType
ACT = mybir.ActivationFunctionType

P = 128
PACK = 4
ROWS = D // PACK
HALF = N // 2
RUN = 2
QUAD = 32
NT = 128


def tile_rows_hvtwogates_kernel(tc, x, w1, w2, w3, th, wo, dy, dx, og, base, out):
    nc = tc.nc

    with ExitStack() as ctx:
        sb = ctx.enter_context(tc.tile_pool(name="sb", bufs=1))
        ps = ctx.enter_context(tc.psum_pool(name="ps", bufs=1))
        ctx.enter_context(tc.manual_schedule())

        def load(name, src, c0, c1):
            raw = sb.tile([P, PACK, c1 - c0], F32, name=name)
            nc.sync.dma_start(out=raw[:], in_=src.rearrange("g (p j) n -> (g p) j n", j=PACK)[:, :, c0:c1])
            return raw

        def operand(name, width):
            rounded = sb.tile([P, width, PACK], BF16, name=name + "_bf", align_bytes=64)
            codes = sb.tile([P, width], U32, name=name + "_codes", align_bytes=64)
            scales = sb.tile([P, width], U8, name=name + "_scales", align_bytes=64)
            return rounded, codes, scales

        def views(op, at, raw, c0, c1):
            dst = op[0][:, at + c0 : at + c1, :].rearrange("p (c i) j -> p c j i", i=RUN)
            src = raw[:, :, c0:c1].rearrange("p j (c i) -> p c j i", i=RUN)
            return dst, src

        def round_v(op, at, raw, c0, c1):
            dst, src = views(op, at, raw, c0, c1)
            nc.vector.tensor_copy(out=dst, in_=src)

        def round_s(op, at, raw, c0, c1):
            dst, src = views(op, at, raw, c0, c1)
            nc.scalar.activation(out=dst, in_=src, func=ACT.Copy)

        def quantise(op, c0, c1):
            nc.vector.quantize_mx(
                out=op[1][:, c0:c1].bitcast(FP8X4),
                scales=op[2][:, c0:c1],
                in_=op[0][:, c0:c1, :].rearrange("p c j -> p (c j)"),
            )

        def product(bank, at, g, w, a):
            rows = slice(g * ROWS, (g + 1) * ROWS)
            for n0 in range(0, a[1].shape[1], NT):
                nc.tensor.matmul_mx(
                    out=bank[g][:, at + n0 : at + n0 + NT],
                    lhsT=w[1][rows, :].bitcast(FP8X4),
                    lhsT_scale=w[2][rows, :],
                    rhs=a[1][rows, n0 : n0 + NT].bitcast(FP8X4),
                    rhs_scale=a[2][rows, n0 : n0 + NT],
                    start=True,
                    stop=True,
                )

        rows_in = sb.tile([P, 2 * G, QUAD], F32, name="rows_in", align_bytes=64)
        cols = sb.tile([P, 2 * G, QUAD], F32, name="cols", align_bytes=64)
        nc.gpsimd.memset(rows_in[:], 0.0)
        for r, vec in enumerate((th, og)):
            nc.scalar.dma_start(
                out=rows_in[0:P:QUAD, r * G : (r + 1) * G, :], in_=vec.rearrange("g (q i) o -> q g (i o)", i=QUAD)
            )
        x0 = load("x0", x, 0, HALF)
        w2r = load("w2r", w2, 0, M)
        dx0 = load("dx0", dx, 0, HALF)
        w3r = load("w3r", w3, 0, M)
        w1r = load("w1r", w1, 0, M)
        x1 = load("x1", x, HALF, N)
        dx1 = load("dx1", dx, HALF, N)
        wor = load("wor", wo, 0, M)
        dyr = load("dyr", dy, 0, N)
        base_sb = sb.tile([P, G, N], F32, name="base_sb")
        nc.sync.dma_start(out=base_sb[:], in_=base.rearrange("g m n -> m g n"))

        bias3 = sb.tile([P, G], F32, name="bias3")
        xq = [operand("x%d" % h, HALF) for h in range(2)]
        dxq = [operand("dx%d" % h, HALF) for h in range(2)]
        w1q, w2q, w3q, woq = [operand(n, M) for n in ("w1", "w2", "w3", "wo")]
        dyq = [operand("dy%d" % h, HALF) for h in range(2)]

        gate_sums, tan3, tan2, values = [
            [ps.tile([P, N], F32, name="%s_%d" % (n, g)) for g in range(G)] for n in ("gate_sums", "tan3", "tan2", "values")
        ]
        bankc = tan3

        def work(name):
            return [sb.tile([P, G, HALF], F32, name="%s_%d" % (name, h)) for h in range(2)]

        t2, t3, sq, va, vb, vc, vd, ve, vf = [work(n) for n in ("t2", "t3", "sq", "va", "vb", "vc", "vd", "ve", "vf")]
        res = sb.tile([P, G, N], F32, name="res")
        fin = sb.tile([P, G, N], F32, name="fin")
        outs = sb.tile([P, G, N], F32, name="outs")
        lo = slice(0, HALF)
        hi = slice(HALF, N)

        def stt(o, a, s, b, op0, op1):
            nc.vector.scalar_tensor_tensor(out=o, in0=a, scalar=s, in1=b, op0=op0, op1=op1)

        def tanh3(h, g):
            nc.scalar.activation(out=t3[h][:, g, :], in_=gate_sums[g][:, lo], func=ACT.Tanh, scale=0.5, bias=bias3[:, g : g + 1])

        def tanh2(h, g):
            nc.scalar.activation(out=t2[h][:, g, :], in_=gate_sums[g][:, hi], func=ACT.Tanh, scale=0.5)

        def squares(h):
            nc.scalar.activation(out=sq[h][:], in_=t2[h][:], func=ACT.Square, scale=0.5)

        def term3(h, gs):
            for g in gs:
                stt(va[h][:, g, :], t3[h][:, g, :], 1.0, tan3[g][:, lo], ALU.subtract, ALU.mult)

        def term2(h, gs):
            for g in gs:
                stt(vb[h][:, g, :], t2[h][:, g, :], 2.0, tan2[g][:, lo], ALU.mult, ALU.mult)

        def term_sum(h):
            nc.vector.tensor_tensor(out=vc[h][:], in0=va[h][:], in1=vb[h][:], op=ALU.add)

        def bracket(h):
            for g in range(G):
                stt(vd[h][:, g, :], vc[h][:, g, :], 0.25, values[g][:, lo], ALU.mult, ALU.mult)
            for g in range(G):
                stt(ve[h][:, g, :], values[g][:, hi], 0.5, vd[h][:, g, :], ALU.mult, ALU.subtract)

        def times_g3(h, gs):
            stt(vf[h][:, gs, :], t3[h][:, gs, :], 1.0, ve[h][:, gs, :], ALU.add, ALU.mult)

        def times_slope(h, gs):
            stt(res[:, gs, h * HALF : (h + 1) * HALF], sq[h][:, gs, :], 0.25, vf[h][:, gs, :], ALU.subtract, ALU.mult)

        SPLIT = 160
        both = slice(0, G)
        round_v(xq[0], 0, x0, 0, SPLIT)
        round_s(xq[0], 0, x0, SPLIT, HALF)
        round_s(w2q, 0, w2r, 0, M)
        quantise(xq[0], 0, HALF)
        quantise(w2q, 0, M)
        for g in range(G):
            product(gate_sums, HALF, g, w2q, xq[0])
        round_v(dxq[0], 0, dx0, 0, SPLIT)
        round_s(dxq[0], 0, dx0, SPLIT, HALF)
        for g in range(G):
            tanh2(0, g)
        squares(0)
        quantise(dxq[0], 0, HALF)
        for g in range(G):
            product(tan2, 0, g, w2q, dxq[0])
        round_v(w3q, 0, w3r, 0, M)
        nc.vector.transpose(out=cols[:].rearrange("p b i -> p (b i)"), in_=rows_in[:].rearrange("p b i -> p (b i)"))
        quantise(w3q, 0, M)
        round_s(w1q, 0, w1r, 0, M)
        nc.scalar.activation(out=bias3[:], in_=cols[:, 0:G, 0], func=ACT.Copy, scale=-0.5)
        for g in range(G):
            product(gate_sums, 0, g, w3q, xq[0])
            product(tan3, 0, g, w3q, dxq[0])
        term2(0, range(G))
        quantise(w1q, 0, M)
        for g in range(G):
            tanh3(0, g)
        for g in range(G):
            product(values, 0, g, w1q, xq[0])
            product(values, HALF, g, w1q, dxq[0])
        term3(0, range(G))
        round_s(xq[1], 0, x1, 0, HALF)
        round_s(dxq[1], 0, dx1, 0, HALF)
        for g in range(G):
            nc.vector.tensor_tensor(out=vc[0][:, g, :], in0=va[0][:, g, :], in1=vb[0][:, g, :], op=ALU.add)
        quantise(xq[1], 0, HALF)
        for g in range(G):
            product(gate_sums, 0, g, w3q, xq[1])
            product(gate_sums, HALF, g, w2q, xq[1])
        bracket(0)
        quantise(dxq[1], 0, HALF)
        for g in range(G):
            product(tan3, 0, g, w3q, dxq[1])
            product(tan2, 0, g, w2q, dxq[1])
        for g in range(G):
            product(values, 0, g, w1q, xq[1])
            product(values, HALF, g, w1q, dxq[1])
        for g in range(G):
            tanh3(1, g)
            tanh2(1, g)
        round_s(woq, 0, wor, 0, M)
        times_g3(0, both)
        for g in range(G):
            term3(1, [g])
            term2(1, [g])
        times_slope(0, both)
        quantise(woq, 0, M)
        for h in range(2):
            round_s(dyq[h], -h * HALF, dyr, h * HALF, (h + 1) * HALF)
        squares(1)
        quantise(dyq[0], 0, HALF)
        for g in range(G):
            product(bankc, 0, g, woq, dyq[0])
        term_sum(1)
        for g in range(G):
            stt(fin[:, g, lo], bankc[g][:, lo], cols[:, G + g, 0:1], res[:, g, lo], ALU.mult, ALU.mult)
            nc.gpsimd.tensor_tensor(out=outs[:, g, lo], in0=base_sb[:, g, lo], in1=fin[:, g, lo], op=ALU.subtract)
        nc.sync.dma_start(out=out.rearrange("g m n -> m g n")[:, :, lo], in_=outs[:, :, lo])
        bracket(1)
        quantise(dyq[1], 0, HALF)
        for g in range(G):
            product(bankc, HALF, g, woq, dyq[1])
        for g in range(G):
            times_g3(1, slice(g, g + 1))
        for g in range(G):
            times_slope(1, slice(g, g + 1))
        for g in range(G):
            stt(fin[:, g, hi], bankc[g][:, hi], cols[:, G + g, 0:1], res[:, g, hi], ALU.mult, ALU.mult)
        for g, queue in ((0, nc.scalar), (1, nc.sync)):
            nc.vector.tensor_tensor(out=outs[:, g, hi], in0=base_sb[:, g, hi], in1=fin[:, g, hi], op=ALU.subtract)
            queue.dma_start(out=out[g, :, hi], in_=outs[:, g, hi])
